import numpy as np, ml_dtypes
CORES = [5,29,101,125,133,157,229,253]
N = 8
import mx_ref
BF = ml_dtypes.bfloat16
def cols(t, e):
    v = np.concatenate([t.reshape(128, -1, 4), np.zeros((128, 1, 4), BF)], axis=1)
    return np.ascontiguousarray(v[:, e]).reshape(128, -1)
def decode(q):
    o = []
    for b in range(4):
        e = np.zeros((128, 128, 4), np.float32); e[np.arange(128), np.arange(128), b] = 1
        o.append(mx_ref.matmul(mx_ref.quantize(e.reshape(128, 512).astype(BF)), q))
    return np.stack(o, axis=2).reshape(128, -1)
def f(rng, *shape):
    return mx_ref.flush((rng.standard_normal(shape, dtype=np.float32) * np.exp2(rng.integers(-2, 3, shape[:-1] + (1,)))).astype(BF))
def wide(rng, *shape, cols=0):
    v = rng.standard_normal(shape, dtype=np.float32) * np.exp2(rng.integers(-12, 13, shape)).astype(np.float32)
    if cols: v *= np.repeat(np.exp2(rng.integers(-cols, cols + 1, shape[:-2] + (1, shape[-1] // 4))) * (rng.random(shape[:-2] + (1, shape[-1] // 4)) > 0.0625), 4, axis=-1).astype(np.float32)
    return mx_ref.flush(v.astype(BF))
K = 384
def plant(t, k, v):
    o = t.astype(np.float32).reshape(128, -1, 4); o[:, k] = v
    return o.reshape(128, -1).astype(BF)
def setup_inputs(rng):
    return {"x": f(rng, N, 128, 512), "c1": f(rng, N, 128, 4 * K), "c2": f(rng, N, 128, 4 * K)}
def setup_inputs_last(rng):
    d = setup_inputs(rng); u = f(rng, 128, 4).astype(np.float32).reshape(128, 1, 4); x = []
    s = np.exp2(np.where(np.arange(128) < 120, 2, 0) + np.arange(128) % 2).astype(np.float32).reshape(1, 128, 1)
    for r in range(N):
        x.append(plant(d["x"][r], rng.permutation(128), u * s))
    d["x"] = np.stack(x)
    for c in ("c1", "c2"):
        d[c] = np.stack([plant(d[c][q], [K - 1], np.float32(2) * u) if q == N - 1 else d[c][q] for q in range(N)])
    return d
def setup_inputs_negative(rng):
    d = setup_inputs(rng)
    for c, s in (("x", 1), ("c1", -1), ("c2", -1)):
        d[c] = (np.abs(d[c].astype(np.float32)) * np.float32(s * 2.0 ** 20)).astype(BF)
    return d
def setup_inputs_own(rng):
    d = setup_inputs(rng)
    for c, s in (("c1", 2), ("c2", -2)):
        d[c] = np.stack([plant(d[c][r], rng.permutation(K)[:128], np.float32(s) * d["x"][r].astype(np.float32).reshape(128, -1, 4)) for r in range(N)])
    return d
def setup_inputs_spread(rng):
    d = setup_inputs(rng); d["x"] = wide(rng, N, 128, 512, cols=8)
    for c in ("c1", "c2"): d[c] = wide(rng, N, 128, 4 * K, cols=2)
    return d
def setup_inputs_ties(rng):
    d = setup_inputs(rng)
    d["x"] = np.stack([plant(d["x"][r], rng.permutation(128)[:1], np.zeros((128, 1, 4), np.float32)) for r in range(N)])
    for c in ("c1", "c2"):
        a = f(rng, N, 128, K)
        d[c] = np.stack([cols(np.concatenate([a[q], a[q], a[(q + 1) % N], a[(q + 2) % N]], axis=1), rng.permutation(K)) for q in range(N)])
    return d
def check_inputs(d):
    b = []
    for c in ("x", "c1", "c2"):
        a = np.abs(d[c].astype(np.float32))
        if not (np.isfinite(a) & ((a == 0) | ((a >= 2.0 ** -30) & (a <= 2.0 ** 30)))).all(): b.append(c)
    return b
def winners(v, book):
    s = np.concatenate([mx_ref.matmul(v, q) for q in book], axis=1)
    w = np.argmax(s + np.float32(0), axis=1)
    return w, s[np.arange(128), w]
def chosen(t, e):
    return t.reshape(128, -1, 4)[:, e].reshape(128, -1)
def reference(x, c1, c2):
    q1 = [mx_ref.quantize(c1[q]) for q in range(N)]
    q2 = [mx_ref.quantize(c2[q]) for q in range(N)]
    d1 = np.concatenate([decode(q) for q in q1], axis=1)
    d2 = np.concatenate([decode(q) for q in q2], axis=1)
    y = np.zeros((N, 128, 512), np.float32); no = np.zeros((N, 4, 128), np.float32)
    for r in range(N):
        w1, s1 = winners(mx_ref.quantize(x[r]), q1)
        R = (x[r].astype(np.float32) - chosen(d1, w1)).astype(BF)
        w2, s2 = winners(mx_ref.quantize(R), q2)
        y[r] = R.astype(np.float32) - chosen(d2, w2)
        no[r, 0] = w1; no[r, 1] = w2; no[r, 2] = s1; no[r, 3] = s2
    return {"y": y, "no": no}

from concourse.bass import DstId, RemoteDMATransfer
from concourse.mybir import dt, AluOpType, AxisListType, ActivationFunctionType

N = 8
K = 384
BIG = -1.0e29
F8 = "float8_e4m3fn_x4"
SCRATCH = {
    "xb": ("sbuf", [128, 512], "bfloat16"), "c1b": ("sbuf", [128, 4 * K], "bfloat16"), "c2b": ("sbuf", [128, 4 * K], "bfloat16"),
    "c1d": ("sbuf", [128, 4 * K], "bfloat16"), "eb": ("sbuf", [128, 2048], "bfloat16"), "h": ("sbuf", [128, 8 * 512], "bfloat16"),
    "rb": ("sbuf", [128, 512], "bfloat16"),
    "xq": ("sbuf", [128, 128], F8), "xp": ("sbuf", [128, 128], "uint8"),
    "xrq": ("sbuf", [128, 128], F8), "xrp": ("sbuf", [128, 128], "uint8"),
    "xsq": ("sbuf", [128, 384], F8), "xsp": ("sbuf", [128, 384], "uint8"),
    "c1q": ("sbuf", [128, K], F8), "c1p": ("sbuf", [128, K], "uint8"),
    "c1sq": ("sbuf", [128, K], F8), "c1sp": ("sbuf", [128, K], "uint8"),
    "c2q": ("sbuf", [128, N * K], F8), "c2p": ("sbuf", [128, N * K], "uint8"),
    "c2sq": ("sbuf", [128, 192], F8), "c2sp": ("sbuf", [128, 192], "uint8"),
    "eq": ("sbuf", [128, 512], F8), "ep": ("sbuf", [128, 512], "uint8"),
    "hq": ("sbuf", [128, 1024], F8), "hp": ("sbuf", [128, 1024], "uint8"),
    "crq": ("sbuf", [128, 256], F8), "crp": ("sbuf", [128, 256], "uint8"),
    "cdq": ("sbuf", [128, 1024], F8), "cdp": ("sbuf", [128, 1024], "uint8"),
    "rq": ("sbuf", [128, 128], F8), "rp": ("sbuf", [128, 128], "uint8"),
    "ew": ("sbuf", [128, 512], "int32"), "mw": ("sbuf", [128, 32], "int32"), "mw2": ("sbuf", [128, 32], "int32"),
    "mask": ("sbuf", [128, 32], "float32"), "rst": ("sbuf", [128, 32], "float32"), "neg": ("sbuf", [128, 512], "float32"),
    "pidx": ("sbuf", [128, 8], "float32"),
    "m": ("sbuf", [128, 3 * K], "float32"), "junk": ("sbuf", [128, 3 * K], "bfloat16"), "val": ("sbuf", [128, 16], "float32"),
    "lb": ("sbuf", [128, 160], "float32"), "lt": ("sbuf", [128, 160], "float32"), "ls": ("sbuf", [128, 160], "float32"),
    "lo": ("sbuf", [128, 40], "uint16"), "sbo": ("sbuf", [128, 16], "float32"),
    "lst": ("sbuf", [128, 64], "uint16"), "sb": ("sbuf", [128, 32], "float32"),
    "sel": ("sbuf", [128, 64], "float32"),
    "dw1": ("sbuf", [128, 4 * 1024], "bfloat16"), "dw2": ("sbuf", [128, 4 * N * K], "bfloat16"),
    "m2": ("sbuf", [128, N * K], "float32"), "junk2": ("sbuf", [128, N * K], "bfloat16"),
    "cnt": ("sbuf", [128, 32], "float32"), "tmp": ("sbuf", [128, 512], "float32"), "yo": ("sbuf", [128, 512], "float32"),
    "ps": ("psum", [128, 4096], "float32"),
}
SEMAPHORES = (["cv", "cs", "ct", "cg", "dx", "dc1", "dc2", "dout", "lsem", "xr", "c1s", "c2b", "sbs"]
              + ["xs%d" % i for i in range(3)] + ["cr%d" % i for i in range(2)]
              + ["l%d" % i for i in range(8)] + ["cd%d" % i for i in range(8)] + ["c2a%d" % i for i in range(8)])
MUL, ADD, MAX, MIN = AluOpType.mult, AluOpType.add, AluOpType.max, AluOpType.min
COPY, SIGN = ActivationFunctionType.Copy, ActivationFunctionType.Sign


def bits(engines):
    return sum(1 << e for e in engines)


def rank_program(g, core, T, topo):
    cores = list(T.cores)
    home = [c for c in topo.cores_of(core) if T.rank_of(c) is not None]
    if not home:
        return
    rc = home[0]
    me = T.rank_of(rc)

    def same(a, b):
        return a == b or topo.same_plane(cores[a], cores[b])

    def pos(a):
        return [b for b in range(N) if same(a, b)].index(a)

    def cross(a):
        return [b for b in range(N) if not same(a, b)]

    def roles(a):
        c = cores[a]
        far = cores[cross(a)[0]]
        ports = [p for p in topo.cores_of(c) if p != c and topo.may_write(p, far)]
        near = [p for p in ports if topo.die(p) == topo.die(c)]
        away = [p for p in ports if topo.die(p) != topo.die(c)]
        rest = [p for p in topo.cores_of(c) if p != c and p not in ports]
        return [near[0], away[0]], [near[1], away[1]], rest

    def kx(a, b):
        return (pos(a) + pos(b)) % 4

    def delta(a, b):
        return (pos(a) - pos(b)) % 4

    def place(a, b):
        return 4 + delta(b, a) if same(a, b) else kx(a, b)

    X = sorted(cross(me), key=lambda b: kx(me, b))
    Y = {delta(b, me): b for b in range(N) if b != me and same(b, me)}
    S, B, W = roles(me)
    likecore = cores[Y[1]]

    eng = {"v": g.vector, "s": g.scalar, "t": g.tensor, "g": g, "y": g.sync}
    cnt = {"v": 0, "s": 0, "t": 0, "g": 0}
    seen = {}
    tot = {}

    def need(q, deps):
        best = {}
        for s, n in deps:
            best[s] = max(best.get(s, 0), n)
        for s in best:
            if seen.get((q, s), 0) < best[s]:
                eng[q].wait_ge(T.sem[s], best[s])
                seen[(q, s)] = best[s]

    def do(q, deps, fn):
        need(q, deps)
        i = fn(eng[q])
        cnt[q] += 1
        i.then_inc(T.sem["c" + q], 1)
        return ("c" + q, cnt[q])

    def load(q, sem, out, in_, deps=()):
        need(q, deps)
        eng[q].dma_start(out, in_).then_inc(T.sem[sem], 16)
        tot[sem] = tot.get(sem, 0) + 16
        return (sem, tot[sem])

    def send(deps, transfers):
        need("g", deps)
        out = []
        for engines, src, dsts, sem in transfers:
            ids = []
            for c, _ in dsts:
                rid, pid = topo.addr(c, core)
                ids.append(DstId(rid=rid, pnc=pid))
            out.append(RemoteDMATransfer(dst_ids=ids, dma_engine_mask=bits(engines), remote_sem=T.sem[sem], srcs=[src], dsts=[d for _, d in dsts]))
            tot["lsem"] = tot.get("lsem", 0) + len(engines)
        g.remote_dma_fused(out, local_sem=T.sem["lsem"])

    def c8(t, a, b):
        return t[:, a:b].bitcast(dt.uint8)

    def send_tiles(deps, items):
        send(deps, [(e, c8(q, a, b), [(c, c8(dq, z, z + b - a)) for c, dq, dp, z in ds], sem) for e, q, p, a, b, ds, sem in items])
        send(deps, [(e, p[:, a:b], [(c, dp[:, z:z + b - a]) for c, dq, dp, z in ds], sem) for e, q, p, a, b, ds, sem in items])

    def finish():
        need("g", [("c" + q, n) for q, n in cnt.items() if n] + [(s, n) for s, n in tot.items()])

    off = topo.engines(core, likecore)
    onchip = topo.engines(core, [c for c in topo.cores_of(core) if c != core][0])
    high = [e for e in onchip if e not in off]

    if core in B or core in W:
        if core in B:
            n, at, dests, arr = 192, 192 * B.index(core), X, 2 * len(off)
        else:
            n, at, dests, arr = 128, 128 * W.index(core), [Y[d] for d in Y], 2 * (len(onchip) // 4)
        col = me * K + at
        send_tiles([("c2b", arr)], [(off, T.c2sq, T.c2sp, 0, n, [(cores[b], T.c2q, T.c2p, col) for b in dests], "c2a%d" % me)])
        finish()
        return

    k_mw = do("g", [], lambda e: e.iota(T.mw[:, :], [[-1, 32]], 128, 1))
    k_neg = do("v", [], lambda e: e.memset(T.neg[:, :], BIG))
    k_r = do("v", [], lambda e: e.memset(T.rst[:, :], 1.0))
    k_r = do("v", [k_r], lambda e: e.memset(T.rst[:, 0:1], 0.0))
    k_r = do("v", [k_r], lambda e: e.memset(T.rst[:, 16:17], 0.0))
    k_m = do("v", [k_mw], lambda e: e.tensor_scalar(T.mw2[:, :], T.mw[:, :], 15, None, AluOpType.bitwise_and))
    k_m = do("v", [k_m], lambda e: e.tensor_scalar(T.mask[:, :], T.mw2[:, :], 0.0, None, AluOpType.is_equal))

    banks = {"n": 0, "free": [[] for _ in range(8)]}

    def product(deps, lq, lp, a, rq, rp, b, n):
        i = banks["n"] % 8
        banks["n"] += 1
        o = T.ps[:, 512 * i:512 * i + n]
        t = do("t", list(deps) + banks["free"][i], lambda e: e.matmul_mx(o, lq[:, a:a + 128], lp[:, a:a + 128], rq[:, b:b + n], rp[:, b:b + n], True, True))
        return i, t

    def build_list(val, deps, i, dst, d):
        f = slice(32 * i, 32 * i + 32)
        t = do("v", list(deps) + [k_m], lambda e: e.tensor_scalar(T.lb[:, f], T.mask[:, :], val, None, MUL))
        t = do("v", [t], lambda e: e.transpose(T.lt[:, f], T.lb[:, f]))
        t = do("v", [t, k_r], lambda e: e.tensor_tensor_scan(T.ls[:, f], T.rst[:, :], T.lt[:, f], 0.0, MUL, ADD))
        for a in range(4):
            u = do("v", [t], lambda e: e.tensor_copy(dst[0:32, d + 2 * a:d + 2 * a + 2], T.ls[32 * a:32 * a + 32, 32 * i + 15:32 * i + 32:16]))
        u = do("v", [u], lambda e: e.tensor_copy(dst[32:64, d:d + 8], dst[0:32, d:d + 8]))
        return do("v", [u], lambda e: e.tensor_copy(dst[64:128, d:d + 8], dst[0:64, d:d + 8]))

    def score(deps, xq, xp, a, cq, cp, i):
        b, t = product(deps, xq, xp, a, cq, cp, 0, K)
        m = T.m[:, K * i:K * i + K]
        ts = do("v", [t, k_neg], lambda e: e.tensor_tensor_scan(m, T.ps[:, 512 * b:512 * b + K], T.neg[:, 0:K], BIG, MAX, MAX))
        banks["free"][b] = [ts]
        tv = do("s", [ts], lambda e: e.activation(T.junk[:, K * i:K * i + K], m, SIGN, bias=T.m[:, K * i + K - 1:K * i + K], scale=-1.0, accum_out=T.val[:, 4 * i:4 * i + 1]))
        return ts, tv

    def tell(i, ts, tv, dst, d):
        do("v", [ts], lambda e: e.tensor_copy(dst[:, d:d + 1], T.m[:, K * i + K - 1:K * i + K]))
        return do("v", [tv], lambda e: e.tensor_scalar(dst[:, d + 1:d + 2], T.val[:, 4 * i:4 * i + 1], float(me * K), None, ADD))

    if core in S:
        s = S.index(core)
        owners = [X[2 * s], X[2 * s + 1], Y[s + 1]]
        e4 = len(off) // 2
        send_tiles([("xr", 2 * len(high))], [(off[e4 * i:e4 * i + e4], T.xrq, T.xrp, 0, 128, [(roles(owners[i])[0][s], T.xsq, T.xsp, 128 * i)], "xs%d" % i) for i in range(2)])
        arr = [2 * e4, 2 * e4, 2 * len(off)]
        c1 = ("c1s", 2 * len(onchip))
        st = {}
        for i in (0, 1):
            st[i] = score([c1, ("xs%d" % i, arr[i])], T.xsq, T.xsp, 128 * i, T.c1sq, T.c1sp, i)
        for i in (0, 1, 2):
            if i == 2:
                st[i] = score([c1, ("xs2", arr[2])], T.xsq, T.xsp, 256, T.c1sq, T.c1sp, 2)
            b = owners[i]
            tl = build_list(T.val[:, 4 * i:4 * i + 1], [st[i][1]], i, T.lo, 8 * i)
            send([tl], [(off, T.lo[:, 8 * i:8 * i + 8], [(rc, T.lst[:, 8 * b:8 * b + 8])], "l%d" % b)])
            tb = tell(i, st[i][0], st[i][1], T.sbo, 4 * i)
            p = 4 * place(b, me)
            send([tb], [(off, T.sbo[:, 4 * i:4 * i + 2], [(cores[b], T.sb[:, p:p + 2])], "sbs")])
        for i in (0, 1):
            b = owners[i]
            p = place(b, me)
            send_tiles([("cr%d" % i, 2 * len(off))], [(off, T.crq, T.crp, 128 * i, 128 * i + 128, [(cores[b], T.cdq, T.cdp, 128 * p)], "cd%d" % p)])
        finish()
        return

    l_x = load("y", "dx", T.xb[:, :], T.x[:, :])
    l_1 = load("s", "dc1", T.c1b[:, :], T.c1[:, :])
    l_2 = load("s", "dc2", T.c2b[:, :], T.c2[:, :])
    k_w = do("g", [], lambda e: e.iota(T.ew[:, :], [[1, 512]], 0, -4))
    k_p = do("g", [], lambda e: e.iota(T.pidx[:, :], [[128, 8]], 0, 1, allow_small_or_imprecise_dtypes=True))
    q_x = do("v", [l_x], lambda e: e.quantize_mx(T.xq[:, :], T.xp[:, :], T.xb[:, :]))
    like = [roles(b)[0][delta(me, b) - 1] if delta(me, b) < 3 else cores[b] for b in Y.values()]
    send_tiles([q_x], [(high, T.xq, T.xp, 0, 128, [(c, T.xrq, T.xrp, 0) for c in S], "xr"),
                       (off, T.xq, T.xp, 0, 128, [(c, T.xsq, T.xsp, 256) for c in like], "xs2")])
    q_1 = do("v", [l_1], lambda e: e.quantize_mx(T.c1q[:, :], T.c1p[:, :], T.c1b[:, :]))
    send_tiles([q_1], [(onchip, T.c1q, T.c1p, 0, K, [(c, T.c1sq, T.c1sp, 0) for c in S], "c1s")])
    for t in range(4):
        k_d = do("s", [l_1], lambda e: e.activation(T.c1d[:, K * t:K * t + K], T.c1b[:, t:4 * K:4], COPY))
    for t in range(4):
        k_e = do("v", [k_w], lambda e: e.tensor_scalar(T.eb[:, 512 * t:512 * t + 512], T.ew[:, :], float(t), None, AluOpType.is_equal))
    k_e = do("v", [k_e], lambda e: e.quantize_mx(T.eq[:, :], T.ep[:, :], T.eb[:, :]))
    o2 = me * K
    q_2 = do("v", [l_2], lambda e: e.quantize_mx(T.c2q[:, o2:o2 + K], T.c2p[:, o2:o2 + K], T.c2b[:, :]))
    send_tiles([q_2], [(e, T.c2q, T.c2p, o2 + 192 * i, o2 + 192 * i + 192, [(B[i], T.c2sq, T.c2sp, 0)], "c2b") for i, e in enumerate([high, off])])
    w4 = len(onchip) // 4
    send_tiles([q_2], [(onchip[w4 * i:w4 * i + w4], T.c2q, T.c2p, o2 + 128 * i, o2 + 128 * i + 128, [(W[i], T.c2sq, T.c2sp, 0)], "c2b") for i in range(3)])

    s_own = score([q_x, q_1], T.xq, T.xp, 0, T.c1q, T.c1p, 0)
    s_3 = score([q_1, ("xs2", 2 * len(off))], T.xsq, T.xsp, 256, T.c1q, T.c1p, 1)
    t_own = build_list(T.val[:, 0:1], [s_own[1]], 0, T.lo, 0)
    t_sb = tell(0, s_own[0], s_own[1], T.sb, 16)
    t_3 = build_list(T.val[:, 4:5], [s_3[1]], 1, T.lo, 8)
    t_sb3 = tell(1, s_3[0], s_3[1], T.sbo, 4)

    def gather(q, lst, a, deps, i):
        for t in range(4):
            o = T.h[:, 512 * i + t:512 * i + 512:4]
            w = T.c1d[:, K * t:K * t + K].indirect(lst[:, a:a + 8])
            if q == "v":
                k = do("v", list(deps) + [k_d], lambda e: e.tensor_copy(o, w))
            else:
                k = do("s", list(deps) + [k_d], lambda e: e.activation(o, w, COPY))
        return k

    ga = gather("s", T.lo, 8, [t_3], 6)
    gb = gather("v", T.lo, 0, [t_own], 7)
    q_own = do("v", [gb], lambda e: e.quantize_mx(T.cdq[:, 512:640], T.cdp[:, 512:640], T.h[:, 7 * 512:8 * 512]))
    q_3 = do("v", [ga], lambda e: e.quantize_mx(T.hq[:, 768:896], T.hp[:, 768:896], T.h[:, 6 * 512:7 * 512]))
    b = Y[3]
    p = place(b, me)
    send([t_sb3], [(off, T.sbo[:, 4:6], [(cores[b], T.sb[:, 4 * p:4 * p + 2])], "sbs")])
    send_tiles([q_3], [(off, T.hq, T.hp, 768, 896, [(cores[b], T.cdq, T.cdp, 128 * p)], "cd%d" % p)])

    NK = N * K
    k_w2 = []

    def decode2(owner, deps):
        for t in range(4):
            i, k = product(list(deps) + [k_e, q_2], T.eq, T.ep, 128 * t, T.c2q, T.c2p, owner * K, K)
            o = T.dw2[:, NK * t + owner * K:NK * t + owner * K + K]
            src = T.ps[:, 512 * i:512 * i + K]
            if t % 2 == 0:
                r = do("v", [k], lambda e: e.tensor_scalar(o, src, -1.0, None, MUL))
            else:
                r = do("s", [k], lambda e: e.activation(o, src, COPY, scale=-1.0))
            banks["free"][i] = [r]
            k_w2.append(r)

    decode2(me, [])
    for i in range(2):
        r0, r1 = X[i], X[2 + i]
        ga = gather("v", T.lst, 8 * r0, [("l%d" % r0, len(off))], 2 * i)
        gb = gather("s", T.lst, 8 * r1, [("l%d" % r1, len(off))], 2 * i + 1)
        z = 256 * i
        q = do("v", [ga, gb], lambda e: e.quantize_mx(T.hq[:, z:z + 256], T.hp[:, z:z + 256], T.h[:, 4 * z:4 * z + 1024]))
        send_tiles([q], [(e, T.hq, T.hp, z + 128 * j, z + 128 * j + 128, [(S[j], T.crq, T.crp, 128 * i)], "cr%d" % i) for j, e in enumerate([high, off])])
    r0, r1 = Y[1], Y[2]
    ga = gather("v", T.lst, 8 * r0, [("l%d" % r0, len(off))], 4)
    gb = gather("s", T.lst, 8 * r1, [("l%d" % r1, len(off))], 5)
    q = do("v", [ga, gb], lambda e: e.quantize_mx(T.hq[:, 512:768], T.hp[:, 512:768], T.h[:, 2048:3072]))
    e4 = len(off) // 2
    send_tiles([q], [(off[e4 * j:e4 * j + e4], T.hq, T.hp, 512 + 128 * j, 640 + 128 * j, [(cores[r], T.cdq, T.cdp, 128 * place(r, me))], "cd%d" % place(r, me)) for j, r in enumerate([r0, r1])])

    for d in (1, 2, 3):
        decode2(Y[d], [("c2a%d" % Y[d], 3 * 2 * len(off))])

    sel = T.sel
    sc, nu = T.sb[:, 0:32:4], T.sb[:, 1:32:4]
    k = do("v", [t_sb, ("sbs", 7 * len(off))], lambda e: e.tensor_reduce(sel[:, 0:1], sc, AxisListType.X, MAX))
    k = do("v", [k], lambda e: e.tensor_scalar(sel[:, 8:16], sc, sel[:, 0:1], 16384.0, AluOpType.is_lt, MUL))
    k = do("v", [k], lambda e: e.tensor_tensor(sel[:, 16:24], sel[:, 8:16], nu, ADD))
    k_n = do("v", [k], lambda e: e.tensor_reduce(sel[:, 1:2], sel[:, 16:24], AxisListType.X, MIN))
    k = do("v", [k_n], lambda e: e.tensor_scalar(sel[:, 24:32], nu, sel[:, 1:2], None, AluOpType.is_equal))
    k = do("v", [k, k_p], lambda e: e.tensor_tensor(sel[:, 32:40], sel[:, 24:32], T.pidx[:, :], MUL))
    k = do("v", [k], lambda e: e.tensor_reduce(sel[:, 2:3], sel[:, 32:40], AxisListType.X, ADD))
    k_l1 = build_list(sel[:, 2:3], [k], 2, T.lo, 16)
    load("y", "dout", T.no[0:1, :], sel[:, 1:2], [k_n])
    load("y", "dout", T.no[2:3, :], sel[:, 0:1], [k_n])

    for b in X:
        decode2(b, [("c2a%d" % b, 2 * 2 * len(off))])

    k_w1 = []

    def decode1(z, deps):
        for t in range(4):
            i, k = product(list(deps) + [k_e], T.eq, T.ep, 128 * t, T.cdq, T.cdp, z, 512)
            o = T.dw1[:, 1024 * t + z:1024 * t + z + 512]
            src = T.ps[:, 512 * i:512 * i + 512]
            if t % 2 == 0:
                r = do("v", [k], lambda e: e.tensor_scalar(o, src, -1.0, None, MUL))
            else:
                r = do("s", [k], lambda e: e.activation(o, src, COPY, scale=-1.0))
            banks["free"][i] = [r]
            k_w1.append(r)

    dl = []
    for b in Y.values():
        dl.append(("cd%d" % place(me, b), 2 * len(off) if delta(me, b) == 3 else len(off)))
    decode1(512, [q_own] + dl)
    decode1(0, [("cd%d" % p, 2 * len(off)) for p in range(4)])

    def winners(win, width, lst, a, deps, base, out):
        ks = {}
        for t in (2, 3):
            w = win[:, width * t:width * t + width].indirect(lst[:, a:a + 8])
            ks[t] = do("s", deps, lambda e: e.activation(T.tmp[:, 128 * t:128 * t + 128], w, COPY))
        for t in (0, 1):
            w = win[:, width * t:width * t + width].indirect(lst[:, a:a + 8])
            k = do("v", deps, lambda e: e.tensor_tensor(out[:, t:512:4], w, base[:, t:512:4], ADD))
        for t in (2, 3):
            k = do("v", [ks[t]], lambda e: e.tensor_tensor(out[:, t:512:4], T.tmp[:, 128 * t:128 * t + 128], base[:, t:512:4], ADD))
        return k

    k_r1 = winners(T.dw1, 1024, T.lo, 16, [k_l1] + k_w1, T.xb, T.rb)
    q_r = do("v", [k_r1], lambda e: e.quantize_mx(T.rq[:, :], T.rp[:, :], T.rb[:, :]))

    n2 = NK // 512
    last = []
    cn = []
    for i in range(n2):
        b, k = product([q_r], T.rq, T.rp, 0, T.c2q, T.c2p, 512 * i, 512)
        z = 512 * i
        ini = BIG if i == 0 else T.m2[:, z - 1:z]
        k = do("v", [k] + last, lambda e: e.tensor_tensor_scan(T.m2[:, z:z + 512], T.ps[:, 512 * b:512 * b + 512], T.neg[:, :], ini, MAX, MAX))
        banks["free"][b] = [k]
        last = [k]
        cn.append(do("s", [k], lambda e: e.activation(T.junk2[:, z:z + 512], T.m2[:, z:z + 512], SIGN, bias=T.m2[:, z + 511:z + 512], scale=-1.0, accum_out=T.cnt[:, i:i + 1])))
    load("y", "dout", T.no[3:4, :], T.m2[:, NK - 1:NK], last)
    k = do("v", last, lambda e: e.tensor_scalar(T.cnt[:, 8:8 + n2], T.m2[:, 511:NK:512], T.m2[:, NK - 1:NK], 512.0, AluOpType.is_lt, MUL))
    k = do("v", [k] + cn, lambda e: e.tensor_tensor(T.cnt[:, 16:16 + n2], T.cnt[:, 8:8 + n2], T.cnt[:, 0:n2], MAX))
    k = do("v", [k], lambda e: e.tensor_reduce(T.cnt[:, 24:25], T.cnt[:, 16:16 + n2], AxisListType.X, ADD))
    load("y", "dout", T.no[1:2, :], T.cnt[:, 24:25], [k])
    k = build_list(T.cnt[:, 24:25], [k], 3, T.lo, 24)
    k = winners(T.dw2, NK, T.lo, 24, [k] + k_w2, T.rb, T.yo)
    load("y", "dout", T.y[:, :], T.yo[:, :], [k])
    finish()
